import numpy as np, ml_dtypes
CORES = [2,3,6,7,58,59,62,63,114,115,118,119]
N = 12
WB, F = 3, 256
def setup_inputs(rng):
    return {"a": rng.standard_normal((N, 128, 128), dtype=np.float32).astype(ml_dtypes.bfloat16), "w": rng.standard_normal((N, 128, F), dtype=np.float32).astype(ml_dtypes.bfloat16)}
def setup_inputs_big(rng):
    d = setup_inputs(rng)
    for k in ("a", "w"): d[k] = (d[k].astype(np.float32) * 1024.0).astype(d[k].dtype)
    return d
def setup_inputs_small(rng):
    d = setup_inputs(rng)
    for k in ("a", "w"): d[k] = (d[k].astype(np.float32) * (1 / 1024.0)).astype(d[k].dtype)
    return d
def setup_inputs_apart(rng):
    d = setup_inputs(rng)
    f = (10.0 ** rng.permutation(np.linspace(-1.5, 1.5, N))).astype(np.float32).reshape(N, 1, 1)
    for k in ("a", "w"): d[k] = (d[k].astype(np.float32) * f).astype(d[k].dtype)
    return d
def reference(a, w):
    A, W = a.astype(np.float64), w.astype(np.float64)
    p = [A[j].T @ W[j] for j in range(N)]
    y = np.stack([sum(p[r - i] for i in range(WB + 1) if r - i >= 0) for r in range(N)])
    return {"y": y.astype(ml_dtypes.bfloat16 if a.dtype != np.float64 else np.float64)}

@@ -1,0 +1,125 @@
+from concourse.bass import DstId, RemoteDMATransfer
+from concourse.mybir import AluOpType
+
+WB = 3
+W = WB + 1
+K, M, F = 128, 128, 256
+
+SCRATCH = {
+    "a_sb": ("sbuf", [K, M], "bfloat16"),
+    "w_sb": ("sbuf", [K, F], "bfloat16"),
+    "p_ps": ("psum", [M, F], "float32"),
+    "p_sb": ("sbuf", [M, F], "bfloat16"),
+    "y_sb": ("sbuf", [M, F], "bfloat16"),
+}
+for _i in range(W):
+    SCRATCH["l%d" % _i] = ("sbuf", [M, F], "bfloat16")
+    SCRATCH["x%d" % _i] = ("sbuf", [M, F], "bfloat16")
+
+SEMAPHORES = ["loaded", "mm", "cp", "acc", "sent", "stored", "sx"] + ["q%d" % _i for _i in range(W)]
+
+
+def _plan(cores, topo):
+    n = len(cores)
+    chip = [topo.chip(c) for c in cores]
+    near = [[] for _ in range(n)]
+    feed = [[] for _ in range(n)]
+    export = [[] for _ in range(n)]
+    for r in range(n):
+        groups = {}
+        for j in range(max(0, r - WB), r):
+            if chip[j] == chip[r]:
+                near[j].append(r)
+            else:
+                groups.setdefault(chip[j], []).append(j)
+        for grp in groups.values():
+            e = [k for k in grp if topo.may_write(cores[k], cores[r])][0]
+            export[e].append((r, grp))
+            for k in grp:
+                if k != e:
+                    feed[k].append(e)
+    return near, feed, export
+
+
+def _mask(topo, cores, src, dsts):
+    m = topo.mask(cores[src], cores[dsts[0]])
+    for d in dsts[1:]:
+        m &= topo.mask(cores[src], cores[d])
+    return m
+
+
+def _count(m):
+    return bin(m).count("1")
+
+
+def rank_program(g, core, T, topo):
+    r = T.rank_of(core)
+    if r is None:
+        return
+    cores = list(T.cores)
+    n = len(cores)
+    near, feed, export = _plan(cores, topo)
+    S = T.sem
+
+    g.sync.dma_start(T.a_sb[:], T.a[:]).then_inc(S.loaded, 16)
+    g.scalar.dma_start(T.w_sb[:], T.w[:]).then_inc(S.loaded, 16)
+    g.tensor.wait_ge(S.loaded, 32)
+    g.tensor.matmul(T.p_ps[:], T.a_sb[:], T.w_sb[:], start=True, stop=True).then_inc(S.mm, 1)
+    v = g.vector
+    v.wait_ge(S.mm, 1)
+    v.tensor_copy(T.p_sb[:], T.p_ps[:]).then_inc(S.cp, 1)
+
+    sent = [0]
+
+    def send(dsts, srcs, buf, sem):
+        m = _mask(topo, cores, r, dsts)
+        ids = []
+        for d in dsts:
+            rid, pid, _se = topo.addr(cores[d])
+            ids.append(DstId(rid=rid, pnc=pid))
+        tr = RemoteDMATransfer(dst_ids=ids, dma_engine_mask=m, remote_sem=sem, srcs=srcs,
+                               dsts=[buf[:] for _ in dsts], alu_op=1 if len(srcs) > 1 else 0)
+        g.remote_dma_fused([tr], local_sem=S.sent)
+        sent[0] += _count(m)
+
+    tag = r % W
+    if feed[r] or near[r] or export[r]:
+        g.wait_ge(S.cp, 1)
+    if feed[r]:
+        send(feed[r], [T.p_sb[:]], T["x%d" % tag], S.sx)
+    if near[r]:
+        send(near[r], [T.p_sb[:]], T["l%d" % tag], S["q%d" % tag])
+    for dst, grp in export[r]:
+        if len(grp) == 1:
+            send([dst], [T.p_sb[:]], T["l%d" % tag], S["q%d" % tag])
+    fed = sum(_count(_mask(topo, cores, k, feed[k])) for k in range(n) if r in feed[k])
+    if fed:
+        g.wait_ge(S.sx, fed)
+    for dst, grp in export[r]:
+        if len(grp) > 1:
+            srcs = [T.p_sb[:]] + [T["x%d" % (k % W)][:] for k in grp if k != r]
+            send([dst], srcs, T["l%d" % tag], S["q%d" % tag])
+
+    inc = [(j, _count(_mask(topo, cores, j, near[j]))) for j in range(n) if r in near[j]]
+    for e in range(n):
+        for dst, grp in export[e]:
+            if dst == r:
+                inc.append((e, _count(_mask(topo, cores, e, [r]))))
+    if inc:
+        v.wait_ge(S.cp, 1)
+    for i, (j, cnt) in enumerate(inc):
+        v.wait_ge(S["q%d" % (j % W)], cnt)
+        if i:
+            v.wait_ge(S.acc, i)
+        out = T.y_sb if i == len(inc) - 1 else T.p_ps
+        v.tensor_tensor(out[:], T.p_ps[:], T["l%d" % (j % W)][:], AluOpType.add).then_inc(S.acc, 1)
+
+    if inc:
+        g.sync.wait_ge(S.acc, len(inc))
+        g.sync.dma_start(T.y[:], T.y_sb[:]).then_inc(S.stored, 16)
+    else:
+        g.sync.wait_ge(S.cp, 1)
+        g.sync.dma_start(T.y[:], T.p_sb[:]).then_inc(S.stored, 16)
+    g.sync.wait_ge(S.stored, 16)
+    if sent[0]:
+        g.wait_ge(S.sent, sent[0])

@@ -4,27 +4,30 @@ from concourse.mybir import AluOpType
 WB = 3
 W = WB + 1
 K, M, F = 128, 128, 256
+BANK = 512
 
 SCRATCH = {
-    "a_sb": ("sbuf", [K, M], "bfloat16"),
-    "w_sb": ("sbuf", [K, F], "bfloat16"),
-    "p_ps": ("psum", [M, F], "float32"),
+    "aw_sb": ("sbuf", [K, M + F], "bfloat16"),
+    "p_ps": ("psum", [M, BANK], "float32"),
+    "y_ps": ("psum", [M, BANK], "float32"),
     "p_sb": ("sbuf", [M, F], "bfloat16"),
     "y_sb": ("sbuf", [M, F], "bfloat16"),
 }
 for _i in range(W):
+    SCRATCH["r%d" % _i] = ("sbuf", [K, M + F], "bfloat16")
     SCRATCH["l%d" % _i] = ("sbuf", [M, F], "bfloat16")
     SCRATCH["x%d" % _i] = ("sbuf", [M, F], "bfloat16")
 
-SEMAPHORES = ["loaded", "mm", "cp", "acc", "sent", "stored", "sx"] + ["q%d" % _i for _i in range(W)]
+SEMAPHORES = ["loaded", "mm", "ymm", "cp", "acc", "sent", "stored", "sx"] + ["q%d" % _i for _i in range(W)]
 
 
 def _plan(cores, topo):
     n = len(cores)
     chip = [topo.chip(c) for c in cores]
     near = [[] for _ in range(n)]
+    far = [[] for _ in range(n)]
     feed = [[] for _ in range(n)]
-    export = [[] for _ in range(n)]
+    fold = [[] for _ in range(n)]
     for r in range(n):
         groups = {}
         for j in range(max(0, r - WB), r):
@@ -33,23 +36,30 @@ def _plan(cores, topo):
             else:
                 groups.setdefault(chip[j], []).append(j)
         for grp in groups.values():
+            if len(grp) == 1:
+                far[grp[0]].append(r)
+                continue
             e = [k for k in grp if topo.may_write(cores[k], cores[r])][0]
-            export[e].append((r, grp))
+            fold[e].append((r, grp))
             for k in grp:
                 if k != e:
                     feed[k].append(e)
-    return near, feed, export
+    return near, far, feed, fold
 
 
-def _mask(topo, cores, src, dsts):
+def _mask(topo, cores, src, dsts, inner=False):
     m = topo.mask(cores[src], cores[dsts[0]])
     for d in dsts[1:]:
         m &= topo.mask(cores[src], cores[d])
-    return m
+    out = m
+    for c in cores:
+        if topo.chip(c) != topo.chip(cores[src]):
+            out &= topo.mask(cores[src], c)
+    return (m & ~out) if inner and (m & ~out) else out
 
 
-def _count(m):
-    return bin(m).count("1")
+def _count(topo, cores, src, dsts, inner=False):
+    return bin(_mask(topo, cores, src, dsts, inner)).count("1")
 
 
 def rank_program(g, core, T, topo):
@@ -58,68 +68,72 @@ def rank_program(g, core, T, topo):
         return
     cores = list(T.cores)
     n = len(cores)
-    near, feed, export = _plan(cores, topo)
+    near, far, feed, fold = _plan(cores, topo)
     S = T.sem
+    tag = r % W
+    need_p = bool(feed[r] or fold[r])
+    raws = [(j, _count(topo, cores, j, near[j])) for j in range(n) if r in near[j]]
+    raws += [(j, _count(topo, cores, j, far[j])) for j in range(n) if r in far[j]]
+    sums = [(e, _count(topo, cores, e, [r])) for e in range(n) for dst, _grp in fold[e] if dst == r]
 
-    g.sync.dma_start(T.a_sb[:], T.a[:]).then_inc(S.loaded, 16)
-    g.scalar.dma_start(T.w_sb[:], T.w[:]).then_inc(S.loaded, 16)
-    g.tensor.wait_ge(S.loaded, 32)
-    g.tensor.matmul(T.p_ps[:], T.a_sb[:], T.w_sb[:], start=True, stop=True).then_inc(S.mm, 1)
-    v = g.vector
-    v.wait_ge(S.mm, 1)
-    v.tensor_copy(T.p_sb[:], T.p_ps[:]).then_inc(S.cp, 1)
+    g.sync.dma_start(T.aw_sb[:, 0:M], T.a[:]).then_inc(S.loaded, 16)
+    g.scalar.dma_start(T.aw_sb[:, M:M + F], T.w[:]).then_inc(S.loaded, 16)
+
+    t = g.tensor
+    t.wait_ge(S.loaded, 32)
+    if need_p:
+        t.matmul(T.p_ps[:, 0:F], T.aw_sb[:, 0:M], T.aw_sb[:, M:M + F], start=True, stop=True).then_inc(S.mm, 1)
+    t.matmul(T.y_ps[:, 0:F], T.aw_sb[:, 0:M], T.aw_sb[:, M:M + F], start=True, stop=not raws).then_inc(S.ymm, 1)
+    for i, (j, cnt) in enumerate(raws):
+        t.wait_ge(S["q%d" % (j % W)], cnt)
+        raw = T["r%d" % (j % W)]
+        t.matmul(T.y_ps[:, 0:F], raw[:, 0:M], raw[:, M:M + F], start=False,
+                 stop=i == len(raws) - 1).then_inc(S.ymm, 1)
 
     sent = [0]
 
-    def send(dsts, srcs, buf, sem):
-        m = _mask(topo, cores, r, dsts)
+    def send(dsts, srcs, buf, sem, inner=False):
         ids = []
         for d in dsts:
             rid, pid, _se = topo.addr(cores[d])
             ids.append(DstId(rid=rid, pnc=pid))
-        tr = RemoteDMATransfer(dst_ids=ids, dma_engine_mask=m, remote_sem=sem, srcs=srcs,
-                               dsts=[buf[:] for _ in dsts], alu_op=1 if len(srcs) > 1 else 0)
+        tr = RemoteDMATransfer(dst_ids=ids, dma_engine_mask=_mask(topo, cores, r, dsts, inner), remote_sem=sem,
+                               srcs=srcs, dsts=[buf[:] for _ in dsts], alu_op=1 if len(srcs) > 1 else 0)
         g.remote_dma_fused([tr], local_sem=S.sent)
-        sent[0] += _count(m)
+        sent[0] += _count(topo, cores, r, dsts, inner)
 
-    tag = r % W
-    if feed[r] or near[r] or export[r]:
+    if far[r] or near[r]:
+        g.wait_ge(S.loaded, 32)
+    if far[r]:
+        send(far[r], [T.aw_sb[:]], T["r%d" % tag], S["q%d" % tag])
+    if near[r]:
+        send(near[r], [T.aw_sb[:]], T["r%d" % tag], S["q%d" % tag])
+    if need_p:
         g.wait_ge(S.cp, 1)
     if feed[r]:
-        send(feed[r], [T.p_sb[:]], T["x%d" % tag], S.sx)
-    if near[r]:
-        send(near[r], [T.p_sb[:]], T["l%d" % tag], S["q%d" % tag])
-    for dst, grp in export[r]:
-        if len(grp) == 1:
-            send([dst], [T.p_sb[:]], T["l%d" % tag], S["q%d" % tag])
-    fed = sum(_count(_mask(topo, cores, k, feed[k])) for k in range(n) if r in feed[k])
+        send(feed[r], [T.p_sb[:]], T["x%d" % tag], S.sx, inner=True)
+    fed = sum(_count(topo, cores, k, feed[k], True) for k in range(n) if r in feed[k])
     if fed:
         g.wait_ge(S.sx, fed)
-    for dst, grp in export[r]:
-        if len(grp) > 1:
-            srcs = [T.p_sb[:]] + [T["x%d" % (k % W)][:] for k in grp if k != r]
-            send([dst], srcs, T["l%d" % tag], S["q%d" % tag])
+    for dst, grp in fold[r]:
+        send([dst], [T.p_sb[:]] + [T["x%d" % (k % W)][:] for k in grp if k != r], T["l%d" % tag], S["q%d" % tag])
 
-    inc = [(j, _count(_mask(topo, cores, j, near[j]))) for j in range(n) if r in near[j]]
-    for e in range(n):
-        for dst, grp in export[e]:
-            if dst == r:
-                inc.append((e, _count(_mask(topo, cores, e, [r]))))
-    if inc:
-        v.wait_ge(S.cp, 1)
-    for i, (j, cnt) in enumerate(inc):
-        v.wait_ge(S["q%d" % (j % W)], cnt)
+    v = g.vector
+    if need_p:
+        v.wait_ge(S.mm, 1)
+        v.tensor_copy(T.p_sb[:], T.p_ps[:, 0:F]).then_inc(S.cp, 1)
+    v.wait_ge(S.ymm, 1 + len(raws))
+    for i, (e, cnt) in enumerate(sums):
+        v.wait_ge(S["q%d" % (e % W)], cnt)
         if i:
             v.wait_ge(S.acc, i)
-        out = T.y_sb if i == len(inc) - 1 else T.p_ps
-        v.tensor_tensor(out[:], T.p_ps[:], T["l%d" % (j % W)][:], AluOpType.add).then_inc(S.acc, 1)
+        out = T.y_sb[:] if i == len(sums) - 1 else T.y_ps[:, 0:F]
+        v.tensor_tensor(out, T.y_ps[:, 0:F], T["l%d" % (e % W)][:], AluOpType.add).then_inc(S.acc, 1)
+    if not sums:
+        v.tensor_copy(T.y_sb[:], T.y_ps[:, 0:F]).then_inc(S.acc, 1)
 
-    if inc:
-        g.sync.wait_ge(S.acc, len(inc))
-        g.sync.dma_start(T.y[:], T.y_sb[:]).then_inc(S.stored, 16)
-    else:
-        g.sync.wait_ge(S.cp, 1)
-        g.sync.dma_start(T.y[:], T.p_sb[:]).then_inc(S.stored, 16)
+    g.sync.wait_ge(S.acc, max(1, len(sums)))
+    g.sync.dma_start(T.y[:], T.y_sb[:]).then_inc(S.stored, 16)
     g.sync.wait_ge(S.stored, 16)
     if sent[0]:
         g.wait_ge(S.sent, sent[0])

@@ -4,11 +4,13 @@ from concourse.mybir import AluOpType
 WB = 3
 W = WB + 1
 K, M, F = 128, 128, 256
+H = F // 2
 BANK = 512
 
 SCRATCH = {
     "aw_sb": ("sbuf", [K, M + F], "bfloat16"),
-    "p_ps": ("psum", [M, BANK], "float32"),
+    "p_ps0": ("psum", [M, BANK], "float32"),
+    "p_ps1": ("psum", [M, BANK], "float32"),
     "y_ps": ("psum", [M, BANK], "float32"),
     "p_sb": ("sbuf", [M, F], "bfloat16"),
     "y_sb": ("sbuf", [M, F], "bfloat16"),
@@ -18,7 +20,8 @@ for _i in range(W):
     SCRATCH["l%d" % _i] = ("sbuf", [M, F], "bfloat16")
     SCRATCH["x%d" % _i] = ("sbuf", [M, F], "bfloat16")
 
-SEMAPHORES = ["loaded", "mm", "ymm", "cp", "acc", "sent", "stored", "sx"] + ["q%d" % _i for _i in range(W)]
+SEMAPHORES = (["la", "lw", "mm0", "mm1", "ymm", "cp", "acc", "sent", "stored", "sx"]
+              + ["q%d" % _i for _i in range(W)] + ["f%d" % _i for _i in range(W)])
 
 
 def _plan(cores, topo):
@@ -28,6 +31,8 @@ def _plan(cores, topo):
     far = [[] for _ in range(n)]
     feed = [[] for _ in range(n)]
     fold = [[] for _ in range(n)]
+    pairs = []
+    port = {}
     for r in range(n):
         groups = {}
         for j in range(max(0, r - WB), r):
@@ -36,30 +41,45 @@ def _plan(cores, topo):
             else:
                 groups.setdefault(chip[j], []).append(j)
         for grp in groups.values():
-            if len(grp) == 1:
-                far[grp[0]].append(r)
-                continue
-            e = [k for k in grp if topo.may_write(cores[k], cores[r])][0]
-            fold[e].append((r, grp))
-            for k in grp:
-                if k != e:
-                    feed[k].append(e)
+            while len(grp) != 2 and grp:
+                j = grp.pop(0)
+                far[j].append(r)
+                port[chip[j], topo.die(cores[j])] = port.get((chip[j], topo.die(cores[j])), 0) + 1
+            if grp:
+                pairs.append((r, grp))
+    for r, grp in pairs:
+        cand = [k for k in range(n) if chip[k] == chip[grp[0]] and topo.may_write(cores[k], cores[r])]
+        e = min(cand, key=lambda k: (port.get((chip[k], topo.die(cores[k])), 0), k not in grp,
+                                     -k if k in grp else sum(k in near[j] for j in range(n))))
+        port[chip[e], topo.die(cores[e])] = port.get((chip[e], topo.die(cores[e])), 0) + 1
+        fold[e].append((r, list(grp)))
+        for k in grp:
+            if k != e and e not in feed[k]:
+                feed[k].append(e)
     return near, far, feed, fold
 
 
-def _mask(topo, cores, src, dsts, inner=False):
-    m = topo.mask(cores[src], cores[dsts[0]])
-    for d in dsts[1:]:
-        m &= topo.mask(cores[src], cores[d])
-    out = m
+def _masks(topo, cores, plan, j):
+    near, far, feed, fold = plan
+    every = None
+    off = None
     for c in cores:
-        if topo.chip(c) != topo.chip(cores[src]):
-            out &= topo.mask(cores[src], c)
-    return (m & ~out) if inner and (m & ~out) else out
+        if c == cores[j]:
+            continue
+        m = topo.mask(cores[j], c)
+        if topo.chip(c) == topo.chip(cores[j]):
+            every = m if every is None else every & m
+        else:
+            off = m if off is None else off & m
+    off &= every
+    inner = every & ~off
+    two = len(feed[j]) == 2 and not far[j]
+    return {"far": off, "near": inner if far[j] else every, "fold": off,
+            "feed": [([feed[j][0]], inner), ([feed[j][1]], off)] if two else [(feed[j], inner)]}
 
 
-def _count(topo, cores, src, dsts, inner=False):
-    return bin(_mask(topo, cores, src, dsts, inner)).count("1")
+def _bits(m):
+    return bin(m).count("1")
 
 
 def rank_program(g, core, T, topo):
@@ -68,21 +88,30 @@ def rank_program(g, core, T, topo):
         return
     cores = list(T.cores)
     n = len(cores)
-    near, far, feed, fold = _plan(cores, topo)
+    plan = _plan(cores, topo)
+    near, far, feed, fold = plan
+    masks = [_masks(topo, cores, plan, j) for j in range(n)]
     S = T.sem
     tag = r % W
-    need_p = bool(feed[r] or fold[r])
-    raws = [(j, _count(topo, cores, j, near[j])) for j in range(n) if r in near[j]]
-    raws += [(j, _count(topo, cores, j, far[j])) for j in range(n) if r in far[j]]
-    sums = [(e, _count(topo, cores, e, [r])) for e in range(n) for dst, _grp in fold[e] if dst == r]
+    need_p = bool(feed[r]) or any(r in grp for _dst, grp in fold[r])
+    calls = [2 if feed[j] else 1 for j in range(n)]
+    raws = [(j, calls[j] * _bits(masks[j]["near"])) for j in range(n) if r in near[j]]
+    raws += [(j, calls[j] * _bits(masks[j]["far"])) for j in range(n) if r in far[j]]
 
-    g.sync.dma_start(T.aw_sb[:, 0:M], T.a[:]).then_inc(S.loaded, 16)
-    g.scalar.dma_start(T.aw_sb[:, M:M + F], T.w[:]).then_inc(S.loaded, 16)
+    def senders(dst):
+        return [e for e in range(n) for d, _grp in fold[e] if d == dst]
+
+    sums = [(i, _bits(masks[e]["fold"])) for i, e in enumerate(senders(r))]
+
+    g.sync.dma_start(T.aw_sb[:, 0:M], T.a[:]).then_inc(S.la, 16)
+    g.scalar.dma_start(T.aw_sb[:, M:M + F], T.w[:]).then_inc(S.lw, 16)
 
     t = g.tensor
-    t.wait_ge(S.loaded, 32)
+    t.wait_ge(S.la, 16)
+    t.wait_ge(S.lw, 16)
     if need_p:
-        t.matmul(T.p_ps[:, 0:F], T.aw_sb[:, 0:M], T.aw_sb[:, M:M + F], start=True, stop=True).then_inc(S.mm, 1)
+        t.matmul(T.p_ps0[:, 0:H], T.aw_sb[:, 0:M], T.aw_sb[:, M:M + H], start=True, stop=True).then_inc(S.mm0, 1)
+        t.matmul(T.p_ps1[:, 0:H], T.aw_sb[:, 0:M], T.aw_sb[:, M + H:M + F], start=True, stop=True).then_inc(S.mm1, 1)
     t.matmul(T.y_ps[:, 0:F], T.aw_sb[:, 0:M], T.aw_sb[:, M:M + F], start=True, stop=not raws).then_inc(S.ymm, 1)
     for i, (j, cnt) in enumerate(raws):
         t.wait_ge(S["q%d" % (j % W)], cnt)
@@ -92,43 +121,53 @@ def rank_program(g, core, T, topo):
 
     sent = [0]
 
-    def send(dsts, srcs, buf, sem, inner=False):
-        ids = []
-        for d in dsts:
-            rid, pid, _se = topo.addr(cores[d])
-            ids.append(DstId(rid=rid, pnc=pid))
-        tr = RemoteDMATransfer(dst_ids=ids, dma_engine_mask=_mask(topo, cores, r, dsts, inner), remote_sem=sem,
-                               srcs=srcs, dsts=[buf[:] for _ in dsts], alu_op=1 if len(srcs) > 1 else 0)
-        g.remote_dma_fused([tr], local_sem=S.sent)
-        sent[0] += _count(topo, cores, r, dsts, inner)
+    def send(parts):
+        trs = []
+        for dsts, srcs, buf, sem, mask in parts:
+            ids = []
+            for d in dsts:
+                rid, pid, _se = topo.addr(cores[d])
+                ids.append(DstId(rid=rid, pnc=pid))
+            trs.append(RemoteDMATransfer(dst_ids=ids, dma_engine_mask=mask, remote_sem=sem, srcs=srcs,
+                                         dsts=[buf for _ in dsts], alu_op=1 if len(srcs) > 1 else 0))
+            sent[0] += _bits(mask)
+        g.remote_dma_fused(trs, local_sem=S.sent)
+
+    def raw_call(lo, hi):
+        send([(dsts, [T.aw_sb[:, lo:hi]], T["r%d" % tag][:, lo:hi], S["q%d" % tag], masks[r][kind])
+              for kind, dsts in (("far", far[r]), ("near", near[r])) if dsts])
 
     if far[r] or near[r]:
-        g.wait_ge(S.loaded, 32)
-    if far[r]:
-        send(far[r], [T.aw_sb[:]], T["r%d" % tag], S["q%d" % tag])
-    if near[r]:
-        send(near[r], [T.aw_sb[:]], T["r%d" % tag], S["q%d" % tag])
+        g.wait_ge(S.la, 16)
+        if calls[r] == 2:
+            raw_call(0, M)
+        g.wait_ge(S.lw, 16)
+        raw_call(M if calls[r] == 2 else 0, M + F)
     if need_p:
-        g.wait_ge(S.cp, 1)
+        g.wait_ge(S.cp, 2)
     if feed[r]:
-        send(feed[r], [T.p_sb[:]], T["x%d" % tag], S.sx, inner=True)
-    fed = sum(_count(topo, cores, k, feed[k], True) for k in range(n) if r in feed[k])
+        send([(dsts, [T.p_sb[:]], T["x%d" % tag][:], S.sx, mask) for dsts, mask in masks[r]["feed"]])
+    fed = sum(_bits(mask) for k in range(n) if feed[k] for dsts, mask in masks[k]["feed"] if r in dsts)
     if fed:
         g.wait_ge(S.sx, fed)
     for dst, grp in fold[r]:
-        send([dst], [T.p_sb[:]] + [T["x%d" % (k % W)][:] for k in grp if k != r], T["l%d" % tag], S["q%d" % tag])
+        i = senders(dst).index(r)
+        send([([dst], [T.p_sb[:] if k == r else T["x%d" % (k % W)][:] for k in grp], T["l%d" % i][:], S["f%d" % i],
+               masks[r]["fold"])])
 
     v = g.vector
     if need_p:
-        v.wait_ge(S.mm, 1)
-        v.tensor_copy(T.p_sb[:], T.p_ps[:, 0:F]).then_inc(S.cp, 1)
+        v.wait_ge(S.mm0, 1)
+        v.tensor_copy(T.p_sb[:, 0:H], T.p_ps0[:, 0:H]).then_inc(S.cp, 1)
+        v.wait_ge(S.mm1, 1)
+        v.tensor_copy(T.p_sb[:, H:F], T.p_ps1[:, 0:H]).then_inc(S.cp, 1)
     v.wait_ge(S.ymm, 1 + len(raws))
-    for i, (e, cnt) in enumerate(sums):
-        v.wait_ge(S["q%d" % (e % W)], cnt)
+    for i, cnt in sums:
+        v.wait_ge(S["f%d" % i], cnt)
         if i:
             v.wait_ge(S.acc, i)
         out = T.y_sb[:] if i == len(sums) - 1 else T.y_ps[:, 0:F]
-        v.tensor_tensor(out, T.y_ps[:, 0:F], T["l%d" % (e % W)][:], AluOpType.add).then_inc(S.acc, 1)
+        v.tensor_tensor(out, T.y_ps[:, 0:F], T["l%d" % i][:], AluOpType.add).then_inc(S.acc, 1)
     if not sums:
         v.tensor_copy(T.y_sb[:], T.y_ps[:, 0:F]).then_inc(S.acc, 1)
 

from concourse.bass import DstId, RemoteDMATransfer
from concourse.mybir import AluOpType

WB = 3
W = WB + 1
K, M, F = 128, 128, 256
H = F // 2
BANK = 512

SCRATCH = {
    "aw_sb": ("sbuf", [K, M + F], "bfloat16"),
    "p_ps0": ("psum", [M, BANK], "float32"),
    "p_ps1": ("psum", [M, BANK], "float32"),
    "y_ps": ("psum", [M, BANK], "float32"),
    "p_sb": ("sbuf", [M, F], "bfloat16"),
    "y_sb": ("sbuf", [M, F], "bfloat16"),
}
for _i in range(W):
    SCRATCH["r%d" % _i] = ("sbuf", [K, M + F], "bfloat16")
    SCRATCH["l%d" % _i] = ("sbuf", [M, F], "bfloat16")
    SCRATCH["x%d" % _i] = ("sbuf", [M, F], "bfloat16")

SEMAPHORES = (["la", "lw", "mm0", "mm1", "ymm", "cp", "acc", "sent", "stored", "sx"]
              + ["q%d" % _i for _i in range(W)] + ["f%d" % _i for _i in range(W)])


def _plan(cores, topo):
    n = len(cores)
    chip = [topo.chip(c) for c in cores]
    near = [[] for _ in range(n)]
    far = [[] for _ in range(n)]
    feed = [[] for _ in range(n)]
    fold = [[] for _ in range(n)]
    pairs = []
    port = {}
    for r in range(n):
        groups = {}
        for j in range(max(0, r - WB), r):
            if chip[j] == chip[r]:
                near[j].append(r)
            else:
                groups.setdefault(chip[j], []).append(j)
        for grp in groups.values():
            while len(grp) != 2 and grp:
                j = grp.pop(0)
                far[j].append(r)
                port[chip[j], topo.die(cores[j])] = port.get((chip[j], topo.die(cores[j])), 0) + 1
            if grp:
                pairs.append((r, grp))
    for r, grp in pairs:
        cand = [k for k in range(n) if chip[k] == chip[grp[0]] and topo.may_write(cores[k], cores[r])]
        e = min(cand, key=lambda k: (port.get((chip[k], topo.die(cores[k])), 0), k not in grp,
                                     -k if k in grp else sum(k in near[j] for j in range(n))))
        port[chip[e], topo.die(cores[e])] = port.get((chip[e], topo.die(cores[e])), 0) + 1
        fold[e].append((r, list(grp)))
        for k in grp:
            if k != e and e not in feed[k]:
                feed[k].append(e)
    return near, far, feed, fold


def _masks(topo, cores, plan, j):
    near, far, feed, fold = plan
    every = None
    off = None
    for c in cores:
        if c == cores[j]:
            continue
        m = topo.mask(cores[j], c)
        if topo.chip(c) == topo.chip(cores[j]):
            every = m if every is None else every & m
        else:
            off = m if off is None else off & m
    off &= every
    inner = every & ~off
    two = len(feed[j]) == 2 and not far[j]
    return {"far": off, "near": inner if far[j] else every, "fold": off,
            "feed": [([feed[j][0]], inner), ([feed[j][1]], off)] if two else [(feed[j], inner)]}


def _bits(m):
    return bin(m).count("1")


def rank_program(g, core, T, topo):
    r = T.rank_of(core)
    if r is None:
        return
    cores = list(T.cores)
    n = len(cores)
    plan = _plan(cores, topo)
    near, far, feed, fold = plan
    masks = [_masks(topo, cores, plan, j) for j in range(n)]
    S = T.sem
    tag = r % W
    need_p = bool(feed[r]) or any(r in grp for _dst, grp in fold[r])
    calls = [2 if feed[j] else 1 for j in range(n)]
    raws = [(j, calls[j] * _bits(masks[j]["near"])) for j in range(n) if r in near[j]]
    raws += [(j, calls[j] * _bits(masks[j]["far"])) for j in range(n) if r in far[j]]

    def senders(dst):
        return [e for e in range(n) for d, _grp in fold[e] if d == dst]

    sums = [(i, _bits(masks[e]["fold"])) for i, e in enumerate(senders(r))]

    g.sync.dma_start(T.aw_sb[:, 0:M], T.a[:]).then_inc(S.la, 16)
    g.scalar.dma_start(T.aw_sb[:, M:M + F], T.w[:]).then_inc(S.lw, 16)

    t = g.tensor
    t.wait_ge(S.la, 16)
    t.wait_ge(S.lw, 16)
    if need_p:
        t.matmul(T.p_ps0[:, 0:H], T.aw_sb[:, 0:M], T.aw_sb[:, M:M + H], start=True, stop=True).then_inc(S.mm0, 1)
        t.matmul(T.p_ps1[:, 0:H], T.aw_sb[:, 0:M], T.aw_sb[:, M + H:M + F], start=True, stop=True).then_inc(S.mm1, 1)
    t.matmul(T.y_ps[:, 0:F], T.aw_sb[:, 0:M], T.aw_sb[:, M:M + F], start=True, stop=not raws).then_inc(S.ymm, 1)
    for i, (j, cnt) in enumerate(raws):
        t.wait_ge(S["q%d" % (j % W)], cnt)
        raw = T["r%d" % (j % W)]
        t.matmul(T.y_ps[:, 0:F], raw[:, 0:M], raw[:, M:M + F], start=False,
                 stop=i == len(raws) - 1).then_inc(S.ymm, 1)

    sent = [0]

    def send(parts):
        trs = []
        for dsts, srcs, buf, sem, mask in parts:
            ids = []
            for d in dsts:
                rid, pid, _se = topo.addr(cores[d])
                ids.append(DstId(rid=rid, pnc=pid))
            trs.append(RemoteDMATransfer(dst_ids=ids, dma_engine_mask=mask, remote_sem=sem, srcs=srcs,
                                         dsts=[buf for _ in dsts], alu_op=1 if len(srcs) > 1 else 0))
            sent[0] += _bits(mask)
        g.remote_dma_fused(trs, local_sem=S.sent)

    def raw_call(lo, hi):
        send([(dsts, [T.aw_sb[:, lo:hi]], T["r%d" % tag][:, lo:hi], S["q%d" % tag], masks[r][kind])
              for kind, dsts in (("far", far[r]), ("near", near[r])) if dsts])

    if far[r] or near[r]:
        g.wait_ge(S.la, 16)
        if calls[r] == 2:
            raw_call(0, M)
        g.wait_ge(S.lw, 16)
        raw_call(M if calls[r] == 2 else 0, M + F)
    if need_p:
        g.wait_ge(S.cp, 2)
    if feed[r]:
        send([(dsts, [T.p_sb[:]], T["x%d" % tag][:], S.sx, mask) for dsts, mask in masks[r]["feed"]])
    fed = sum(_bits(mask) for k in range(n) if feed[k] for dsts, mask in masks[k]["feed"] if r in dsts)
    if fed:
        g.wait_ge(S.sx, fed)
    for dst, grp in fold[r]:
        i = senders(dst).index(r)
        send([([dst], [T.p_sb[:] if k == r else T["x%d" % (k % W)][:] for k in grp], T["l%d" % i][:], S["f%d" % i],
               masks[r]["fold"])])

    v = g.vector
    if need_p:
        v.wait_ge(S.mm0, 1)
        v.tensor_copy(T.p_sb[:, 0:H], T.p_ps0[:, 0:H]).then_inc(S.cp, 1)
        v.wait_ge(S.mm1, 1)
        v.tensor_copy(T.p_sb[:, H:F], T.p_ps1[:, 0:H]).then_inc(S.cp, 1)
    v.wait_ge(S.ymm, 1 + len(raws))
    for i, cnt in sums:
        v.wait_ge(S["f%d" % i], cnt)
        if i:
            v.wait_ge(S.acc, i)
        out = T.y_sb[:] if i == len(sums) - 1 else T.y_ps[:, 0:F]
        v.tensor_tensor(out, T.y_ps[:, 0:F], T["l%d" % i][:], AluOpType.add).then_inc(S.acc, 1)
    if not sums:
        v.tensor_copy(T.y_sb[:], T.y_ps[:, 0:F]).then_inc(S.acc, 1)

    g.sync.wait_ge(S.acc, max(1, len(sums)))
    g.sync.dma_start(T.y[:], T.y_sb[:]).then_inc(S.stored, 16)
    g.sync.wait_ge(S.stored, 16)
    if sent[0]:
        g.wait_ge(S.sent, sent[0])
